import numpy as np
import ml_dtypes


def mxq(x, axis, fmt="e4m3"):
    dtype, down = {"e4m3": (ml_dtypes.float8_e4m3fn, 7), "e5m2": (ml_dtypes.float8_e5m2, 14)}[fmt]
    v = np.moveaxis(np.asarray(x, np.float32).astype(ml_dtypes.bfloat16).astype(np.float64), axis, -1)
    blocks = v.reshape(v.shape[:-1] + (-1, 32))
    amax = np.abs(blocks).max(-1, keepdims=True)
    byte = np.maximum(np.where(amax > 0, np.frexp(amax)[1] - 1 + 127, 0) - down, 1)
    scale = np.exp2(byte - 127.0)
    codes = (blocks / scale).astype(np.float32).astype(dtype).astype(np.float64)
    return np.moveaxis((codes * scale).reshape(v.shape), -1, axis)


WIDE = False


def mx_kscale(k):
    if not WIDE:
        return np.ones(k)
    levels = np.array([10, -10, 5, -5, 0])
    if k % 512:
        return np.exp2(np.random.permutation(np.resize(levels, k // 32))).repeat(32)
    a = np.empty((k // 512, 16))
    for p in range(k // 512):
        a[p, :8] = np.random.permutation(np.resize(levels, 8))
        for g in range(8):
            far = levels[np.abs(levels - a[p, g]) >= 10]
            a[p, g + 8] = far[np.random.randint(len(far))]
    return np.exp2(a.ravel()).repeat(32)


BF16 = ml_dtypes.bfloat16


def bf(x):
    return np.asarray(x, np.float32).astype(BF16)


def f64(x):
    return np.asarray(x).astype(np.float64)


E2M1 = np.array([0.0, 0.5, 1.0, 1.5, 2.0, 3.0, 4.0, 6.0, -0.0, -0.5, -1.0, -1.5, -2.0, -3.0, -4.0, -6.0])


def pack_weight(w, fmt):
    k, n = w.shape
    w = f64(bf(w)).reshape(k // 32, 32, n)
    amax = np.abs(w).max(1)
    if fmt == "e4m3":
        byte = np.frexp(amax)[1] - 1 + 127 - 7
    else:
        mant, ex = np.frexp(amax / 6.0)
        byte = np.where(mant > 0.5, ex, ex - 1) + 127
    byte = np.clip(np.where(amax > 0, byte, 1), 1, 254)
    scaled = (w * np.exp2(127.0 - byte)[:, None, :]).reshape(k, n).astype(np.float32)
    by_word = np.ascontiguousarray(scaled.reshape(k // 512, 128, 4, n).transpose(0, 1, 3, 2))
    if fmt == "e4m3":
        words = by_word.astype(ml_dtypes.float8_e4m3fn).view(np.uint8)
    else:
        c = by_word.astype(ml_dtypes.float4_e2m1fn).view(np.uint8) & 0xF
        words = c[..., 0::2] | (c[..., 1::2] << 4)
    return np.ascontiguousarray(words), np.ascontiguousarray(byte.astype(np.uint8).reshape(k // 512, 16, n))


def unpack_weight(words, scales, fmt):
    g, p, n, _ = words.shape
    if fmt == "e4m3":
        vals = np.ascontiguousarray(words).view(ml_dtypes.float8_e4m3fn).astype(np.float64)
    else:
        nib = np.empty((g, p, n, 4), np.uint8)
        nib[..., 0::2] = words & 0xF
        nib[..., 1::2] = words >> 4
        vals = E2M1[nib]
    vals = vals * np.repeat(np.exp2(scales.astype(np.float64) - 127.0), 8, axis=1)[..., None]
    return vals.transpose(0, 1, 3, 2).reshape(g * 512, n)
def pack4(w):
    words, scales = pack_weight(w, "e2m1")
    return words.reshape(words.shape[0], 128, -1), scales


def unpack4(words, scales):
    return unpack_weight(words.reshape(words.shape[0], 128, -1, 2), scales, "e2m1")


P, K, Q, F = 2048, 1024, 512, 1024
DELTA_LO, DELTA_HI = 0.05, 0.45
IPW_LO, IPW_HI = 0.5, 2.0


def draw0():
    s = mx_kscale(K)
    t = mx_kscale(P)
    d = bf(np.random.standard_normal((P, K)) * s)
    v = bf(np.random.standard_normal((K, Q)) / np.sqrt(K) / s[:, None])
    delta = bf(np.random.uniform(DELTA_LO, DELTA_HI, (P, Q)) * t[:, None])
    ipw = bf(np.random.uniform(IPW_LO, IPW_HI, P) / t)
    e_words, e_scales = pack4(np.random.standard_normal((K, F)) / np.sqrt(K) / s[:, None])
    return {"d": d, "v": v, "delta": delta, "ipw": ipw,
            "e_words": e_words, "e_scales": e_scales}


def core(d, v, delta, ipw, e_words, e_scales):
    dq = mxq(f64(d), 1, "e4m3")
    diff = dq @ mxq(f64(v), 0, "e4m3")
    lam = f64(delta) / (1.0 + np.exp(diff))
    h = (dq @ unpack4(e_words, e_scales)) * f64(ipw)[:, None]
    return mxq(lam, 0, "e4m3").T @ mxq(h, 0, "e4m3")


def e4m3fn_bytes(y):
    return np.clip(np.asarray(y, np.float64), -448.0, 448.0).astype(np.float32).astype(ml_dtypes.float8_e4m3fn).view(np.uint8)


def e4m3fn_values(b):
    return np.asarray(b, np.uint8).view(ml_dtypes.float8_e4m3fn).astype(np.float64)


def setup_inputs():
    d = draw0()
    x0 = np.asarray(d['d']).astype(np.float64)
    s = (np.max(np.abs(x0), axis=(0,), keepdims=True) / 448.0).astype(np.float32)
    out = {}
    for k, v in d.items():
        if k == 'd':
            out['d_bytes'] = e4m3fn_bytes(x0 / s.astype(np.float64))
            out['d_scale'] = s
        else:
            out[k] = v
    return out


def reference(d_bytes, d_scale, v, delta, ipw, e_words, e_scales):
    return core(e4m3fn_values(d_bytes) * d_scale.astype(np.float64), v, delta, ipw, e_words, e_scales)

@@ -1,0 +1,273 @@
+from contextlib import ExitStack
+
+import concourse.mybir as mybir
+from concourse.masks import make_identity
+
+F32 = mybir.dt.float32
+BF16 = mybir.dt.bfloat16
+I32 = mybir.dt.int32
+U32 = mybir.dt.uint32
+U8 = mybir.dt.uint8
+FP8 = mybir.dt.float8_e4m3fn
+E4M3X4 = mybir.dt.float8_e4m3fn_x4
+E2M1X4 = mybir.dt.float4_e2m1fn_x4
+MULT = mybir.AluOpType.mult
+COPY = mybir.ActivationFunctionType.Copy
+SIGMOID = mybir.ActivationFunctionType.Sigmoid
+
+PAIRS, RAW, RANKERS, FEATS = 2048, 1024, 512, 1024
+P = 128
+PACK = 4
+GROUP = P * PACK
+GROUPS = PAIRS // GROUP
+PASSES = RAW // GROUP
+HALVES = FEATS // 512
+TILES = PAIRS // P
+QTILES = RANKERS // P
+
+FLOPS = 2 * PAIRS * RAW * RANKERS + 2 * PAIRS * RAW * FEATS + 2 * RANKERS * PAIRS * FEATS
+
+
+def tile_lambdarank_head_gradient_s11_kernel(tc, d_bytes, d_scale, v, delta, ipw, e_words, e_scales, out):
+    nc = tc.nc
+    with ExitStack() as ctx:
+        keep = ctx.enter_context(tc.tile_pool(name="keep", bufs=1))
+        work = ctx.enter_context(tc.tile_pool(name="work", bufs=3))
+        psum = ctx.enter_context(tc.psum_pool(name="psum", bufs=1))
+
+        ident = keep.tile([P, P], F32, name="ident")
+        make_identity(nc, ident[:])
+
+        ctx.enter_context(tc.manual_schedule())
+
+        scale_bc = keep.tile([P, RAW], F32, name="scale_bc", align_bytes=64)
+        raw = [keep.tile([P, PACK, RAW], U8, name=f"raw{s}", align_bytes=64) for s in range(GROUPS)]
+        dlt = [keep.tile([P, PACK, RANKERS], BF16, name=f"dlt{s}", align_bytes=64) for s in range(GROUPS)]
+        v_raw = [keep.tile([P, PACK, RANKERS], BF16, name=f"v_raw{g}", align_bytes=64) for g in range(PASSES)]
+        e_w = [keep.tile([P, 2 * FEATS], U8, name=f"e_w{g}", align_bytes=64) for g in range(PASSES)]
+        e_s = keep.tile([P, PASSES, FEATS], U8, name="e_s", align_bytes=64)
+        ipw_bf = keep.tile([P, GROUPS, PACK], BF16, name="ipw_bf")
+        ipw_f = keep.tile([P, GROUPS, PACK], F32, name="ipw_f")
+
+        warm = keep.tile([P, 1], F32, name="warm")
+        nc.vector.memset(warm[:], 0.0)
+        warm_out = keep.tile([P, 1], F32, name="warm_out")
+        nc.scalar.activation(out=warm_out[:], in_=warm[:], func=SIGMOID, scale=-1.0)
+        nc.vector.memset(e_s[:].bitcast(I32), 0)
+
+        d_view = d_bytes.rearrange("(s m t) k -> s m t k", m=P, t=PACK)
+        dlt_view = delta.rearrange("(s m t) q -> s m t q", m=P, t=PACK)
+        v_view = v.rearrange("(g p t) n -> g p t n", p=P, t=PACK)
+        s_view = e_scales.rearrange("g r n -> r g n")
+
+        nc.sync.dma_start(out=scale_bc[:], in_=d_scale.rearrange("o k -> (o k)").partition_broadcast(P))
+        nc.sync.dma_start(out=raw[0][:], in_=d_view[0])
+        for g in range(PASSES):
+            nc.sync.dma_start(out=v_raw[g][:], in_=v_view[g])
+        for g in range(PASSES):
+            nc.sync.dma_start(out=e_w[g][:], in_=e_words[g])
+        for quad in range(4):
+            nc.sync.dma_start(out=e_s[32 * quad : 32 * quad + 4].bitcast(I32), in_=s_view[4 * quad : 4 * quad + 4].bitcast(I32))
+        nc.sync.dma_start(out=ipw_bf[:], in_=ipw.rearrange("(s m t) -> m s t", m=P, t=PACK))
+        nc.sync.dma_start(out=raw[1][:], in_=d_view[1])
+        nc.sync.dma_start(out=dlt[0][:], in_=dlt_view[0])
+        nc.sync.dma_start(out=raw[2][:], in_=d_view[2])
+        nc.sync.dma_start(out=dlt[1][:], in_=dlt_view[1])
+        nc.sync.dma_start(out=raw[3][:], in_=d_view[3])
+        nc.sync.dma_start(out=dlt[2][:], in_=dlt_view[2])
+        nc.sync.dma_start(out=dlt[3][:], in_=dlt_view[3])
+
+        v_codes = [keep.tile([P, RANKERS], U32, name=f"v_codes{g}", align_bytes=64) for g in range(PASSES)]
+        v_planes = [keep.tile([P, RANKERS], U8, name=f"v_planes{g}", align_bytes=64) for g in range(PASSES)]
+        v_grp = [keep.tile([P, RANKERS, PACK], BF16, name=f"v_grp{g}", align_bytes=64) for g in range(PASSES)]
+
+        def v_interleave(g):
+            nc.scalar.copy(
+                out=v_grp[g][:].rearrange("p (c i) t -> p c t i", i=4),
+                in_=v_raw[g][:].rearrange("p t (c i) -> p c t i", i=4),
+            )
+
+        def v_quantize(g):
+            nc.vector.quantize_mx(
+                out=v_codes[g][:].bitcast(E4M3X4), scales=v_planes[g][:], in_=v_grp[g][:].rearrange("p n t -> p (n t)")
+            )
+
+        d_codes = [keep.tile([P, PASSES * P], U32, name=f"d_codes{j}", align_bytes=64) for j in range(TILES)]
+        d_planes = [keep.tile([P, PASSES * P], U8, name=f"d_planes{j}", align_bytes=64) for j in range(TILES)]
+        scaled, turned, grouped = {}, {}, {}
+
+        def widen(j):
+            scaled[j] = work.tile([P, RAW], BF16, name="scaled", align_bytes=64)
+            nc.vector.tensor_tensor(
+                out=scaled[j][:], in0=raw[j // PACK][:, j % PACK, :].bitcast(FP8), in1=scale_bc[:], op=MULT
+            )
+
+        def turn(j):
+            turned[j] = psum.tile([P, PASSES, 2, P], F32, name="tp")
+            words = scaled[j][:].bitcast(F32)
+            for g in range(PASSES):
+                for u in range(2):
+                    nc.tensor.transpose(turned[j][:, g, u, :], words[:, 256 * g + u : 256 * (g + 1) : 2], ident[:])
+
+        def gather(j):
+            grouped[j] = work.tile([P, PASSES * P * PACK], BF16, name="grouped", align_bytes=64)
+            nc.scalar.copy(
+                out=grouped[j][:].bitcast(F32).rearrange("p (g r u) -> p g r u", g=PASSES, u=2),
+                in_=turned[j][:].rearrange("p g u r -> p g r u"),
+            )
+
+        def d_quantize(j):
+            nc.vector.quantize_mx(out=d_codes[j][:].bitcast(E4M3X4), scales=d_planes[j][:], in_=grouped[j][:])
+
+        diff, enc = {}, {}
+        sig, h_raw = {}, {}
+
+        def score(j):
+            diff[j] = psum.tile([P, RANKERS], F32, name="df")
+            for g in range(PASSES):
+                cols = slice(g * P, (g + 1) * P)
+                nc.tensor.matmul_mx(
+                    out=diff[j][:], lhsT=d_codes[j][:, cols].bitcast(E4M3X4), lhsT_scale=d_planes[j][:, cols],
+                    rhs=v_codes[g][:].bitcast(E4M3X4), rhs_scale=v_planes[g][:], start=(g == 0), stop=(g == PASSES - 1),
+                )
+
+        def sigmoid(j):
+            s, t = divmod(j, PACK)
+            if t == 0:
+                sig[s] = work.tile([P, PACK, RANKERS], F32, name="sig", bufs=2, align_bytes=64)
+            nc.scalar.activation(out=sig[s][:, t, :], in_=diff[j][:], func=SIGMOID, scale=-1.0)
+
+        def encode(j, half):
+            enc[j, half] = psum.tile([P, 512], F32, name=f"en{half}")
+            for g in range(PASSES):
+                cols = slice(g * P, (g + 1) * P)
+                nc.tensor.matmul_mx(
+                    out=enc[j, half][:], lhsT=d_codes[j][:, cols].bitcast(E4M3X4), lhsT_scale=d_planes[j][:, cols],
+                    rhs=e_w[g][:, 1024 * half : 1024 * (half + 1)].bitcast(E2M1X4), rhs_scale=e_s[:, g, 512 * half : 512 * (half + 1)],
+                    start=(g == 0), stop=(g == PASSES - 1),
+                )
+
+        def weigh(j, half):
+            s, t = divmod(j, PACK)
+            if t == 0:
+                h_raw[s, half] = work.tile([P, PACK, 512], BF16, name=f"h_raw{half}", bufs=2, align_bytes=64)
+            nc.scalar.activation(out=h_raw[s, half][:, t, :], in_=enc[j, half][:], func=COPY, scale=ipw_f[:, s, t : t + 1])
+
+        lam_codes = [keep.tile([P, RANKERS], U32, name=f"lam_codes{s}", align_bytes=64) for s in range(GROUPS)]
+        lam_planes = [keep.tile([P, RANKERS], U8, name=f"lam_planes{s}", align_bytes=64) for s in range(GROUPS)]
+        h_codes = {(s, h): keep.tile([P, 512], U32, name=f"h_codes{s}_{h}", align_bytes=64) for s in range(GROUPS) for h in range(HALVES)}
+        h_planes = {(s, h): keep.tile([P, 512], U8, name=f"h_planes{s}_{h}", align_bytes=64) for s in range(GROUPS) for h in range(HALVES)}
+        lam, h_grp = {}, {}
+
+        def lam_mult(s, part):
+            if part == 0:
+                lam[s] = work.tile([P, RANKERS, PACK], BF16, name="lam", bufs=2, align_bytes=64)
+            cols = slice(256 * part, 256 * (part + 1))
+            nc.vector.tensor_tensor(
+                out=lam[s][:, cols, :].rearrange("p (c i) t -> p c t i", i=4),
+                in0=sig[s][:, :, cols].rearrange("p t (c i) -> p c t i", i=4),
+                in1=dlt[s][:, :, cols].rearrange("p t (c i) -> p c t i", i=4),
+                op=MULT,
+            )
+
+        def lam_quantize(s):
+            nc.vector.quantize_mx(
+                out=lam_codes[s][:].bitcast(E4M3X4), scales=lam_planes[s][:], in_=lam[s][:].rearrange("p n t -> p (n t)")
+            )
+
+        def h_interleave(s, half):
+            h_grp[s, half] = work.tile([P, 512, PACK], BF16, name="h_grp", bufs=2, align_bytes=64)
+            nc.vector.tensor_copy(
+                out=h_grp[s, half][:].rearrange("p (c i) t -> p c t i", i=4),
+                in_=h_raw[s, half][:].rearrange("p t (c i) -> p c t i", i=4),
+            )
+
+        def h_quantize(s, half):
+            nc.vector.quantize_mx(
+                out=h_codes[s, half][:].bitcast(E4M3X4), scales=h_planes[s, half][:],
+                in_=h_grp[s, half][:].rearrange("p n t -> p (n t)"),
+            )
+
+        acc = {}
+        late_banks = ("tp", "df", "en0", "en1")
+
+        def update(s, half, m):
+            if s == 0:
+                acc[half, m] = psum.tile([P, 512], F32, name=f"acc{m}" if half == 0 else late_banks[m])
+            cols = slice(m * P, (m + 1) * P)
+            nc.tensor.matmul_mx(
+                out=acc[half, m][:], lhsT=lam_codes[s][:, cols].bitcast(E4M3X4), lhsT_scale=lam_planes[s][:, cols],
+                rhs=h_codes[s, half][:].bitcast(E4M3X4), rhs_scale=h_planes[s, half][:], start=(s == 0), stop=(s == GROUPS - 1),
+            )
+
+        def store(half, m, engine):
+            res = work.tile([P, 512], F32, name="res", bufs=4)
+            if engine == "scalar":
+                nc.scalar.copy(out=res[:], in_=acc[half, m][:])
+            else:
+                nc.vector.tensor_copy(out=res[:], in_=acc[half, m][:])
+            nc.sync.dma_start(out=out[m * P : (m + 1) * P, 512 * half : 512 * (half + 1)], in_=res[:])
+
+        widen(0)
+        turn(0)
+        gather(0)
+        widen(1)
+        v_interleave(0)
+        nc.vector.tensor_copy(out=ipw_f[:], in_=ipw_bf[:])
+        d_quantize(0)
+        v_interleave(1)
+        v_quantize(0)
+        for j in range(TILES):
+            prev = j // PACK - 1
+            t = j % PACK
+            if j + 2 < TILES:
+                widen(j + 2)
+            if j == 0:
+                v_quantize(1)
+            if j + 1 < TILES:
+                turn(j + 1)
+                gather(j + 1)
+            score(j)
+            sigmoid(j)
+            for half in range(HALVES):
+                encode(j, half)
+                weigh(j, half)
+            if prev >= 0:
+                if t == 0:
+                    lam_mult(prev, 0)
+                elif t == 1:
+                    lam_quantize(prev)
+                elif t == 2:
+                    h_quantize(prev, 0)
+                else:
+                    h_quantize(prev, 1)
+                    for m in range(QTILES):
+                        update(prev, 0, m)
+            if j + 1 < TILES:
+                d_quantize(j + 1)
+            if prev >= 0:
+                if t == 0:
+                    lam_mult(prev, 1)
+                elif t == 1:
+                    h_interleave(prev, 0)
+                elif t == 2:
+                    h_interleave(prev, 1)
+        last = GROUPS - 1
+        for m in range(QTILES):
+            for s in range(last):
+                update(s, 1, m)
+        lam_mult(last, 0)
+        lam_mult(last, 1)
+        h_interleave(last, 0)
+        lam_quantize(last)
+        h_interleave(last, 1)
+        h_quantize(last, 0)
+        for m in range(QTILES):
+            update(last, 0, m)
+        h_quantize(last, 1)
+        for m in range(QTILES):
+            update(last, 1, m)
+        for m in range(QTILES):
+            store(0, m, "scalar")
+        for m in range(QTILES):
+            store(1, m, "vector" if m % 2 == 0 else "scalar")

@@ -60,31 +60,32 @@ def tile_lambdarank_head_gradient_s11_kernel(tc, d_bytes, d_scale, v, delta, ipw
         v_view = v.rearrange("(g p t) n -> g p t n", p=P, t=PACK)
         s_view = e_scales.rearrange("g r n -> r g n")
 
-        nc.sync.dma_start(out=scale_bc[:], in_=d_scale.rearrange("o k -> (o k)").partition_broadcast(P))
-        nc.sync.dma_start(out=raw[0][:], in_=d_view[0])
-        for g in range(PASSES):
-            nc.sync.dma_start(out=v_raw[g][:], in_=v_view[g])
+        nc.sync.dma_start(out=v_raw[0][:], in_=v_view[0])
+        nc.scalar.dma_start(out=scale_bc[:], in_=d_scale.rearrange("o k -> (o k)").partition_broadcast(P))
+        nc.sync.dma_start(out=raw[0][:, 0, :], in_=d_view[0][:, 0, :])
+        nc.sync.dma_start(out=raw[0][:, 1:, :], in_=d_view[0][:, 1:, :])
         for g in range(PASSES):
             nc.sync.dma_start(out=e_w[g][:], in_=e_words[g])
         for quad in range(4):
             nc.sync.dma_start(out=e_s[32 * quad : 32 * quad + 4].bitcast(I32), in_=s_view[4 * quad : 4 * quad + 4].bitcast(I32))
         nc.sync.dma_start(out=ipw_bf[:], in_=ipw.rearrange("(s m t) -> m s t", m=P, t=PACK))
+        nc.sync.dma_start(out=v_raw[1][:], in_=v_view[1])
         nc.sync.dma_start(out=raw[1][:], in_=d_view[1])
-        nc.sync.dma_start(out=dlt[0][:], in_=dlt_view[0])
         nc.sync.dma_start(out=raw[2][:], in_=d_view[2])
-        nc.sync.dma_start(out=dlt[1][:], in_=dlt_view[1])
+        nc.sync.dma_start(out=dlt[0][:], in_=dlt_view[0])
         nc.sync.dma_start(out=raw[3][:], in_=d_view[3])
-        nc.sync.dma_start(out=dlt[2][:], in_=dlt_view[2])
-        nc.sync.dma_start(out=dlt[3][:], in_=dlt_view[3])
+        for s in range(1, GROUPS):
+            nc.sync.dma_start(out=dlt[s][:], in_=dlt_view[s])
 
         v_codes = [keep.tile([P, RANKERS], U32, name=f"v_codes{g}", align_bytes=64) for g in range(PASSES)]
         v_planes = [keep.tile([P, RANKERS], U8, name=f"v_planes{g}", align_bytes=64) for g in range(PASSES)]
         v_grp = [keep.tile([P, RANKERS, PACK], BF16, name=f"v_grp{g}", align_bytes=64) for g in range(PASSES)]
 
-        def v_interleave(g):
-            nc.scalar.copy(
-                out=v_grp[g][:].rearrange("p (c i) t -> p c t i", i=4),
-                in_=v_raw[g][:].rearrange("p t (c i) -> p c t i", i=4),
+        def v_interleave(g, part, parts, copy):
+            cols = slice(RANKERS // parts * part, RANKERS // parts * (part + 1))
+            copy(
+                out=v_grp[g][:, cols, :].rearrange("p (c i) t -> p c t i", i=4),
+                in_=v_raw[g][:, :, cols].rearrange("p t (c i) -> p c t i", i=4),
             )
 
         def v_quantize(g):
@@ -97,13 +98,13 @@ def tile_lambdarank_head_gradient_s11_kernel(tc, d_bytes, d_scale, v, delta, ipw
         scaled, turned, grouped = {}, {}, {}
 
         def widen(j):
-            scaled[j] = work.tile([P, RAW], BF16, name="scaled", align_bytes=64)
+            scaled[j] = work.tile([P, RAW], BF16, name="scaled", bufs=9, align_bytes=64)
             nc.vector.tensor_tensor(
                 out=scaled[j][:], in0=raw[j // PACK][:, j % PACK, :].bitcast(FP8), in1=scale_bc[:], op=MULT
             )
 
         def turn(j):
-            turned[j] = psum.tile([P, PASSES, 2, P], F32, name="tp")
+            turned[j] = psum.tile([P, PASSES, 2, P], F32, name=f"tp{j % 2}")
             words = scaled[j][:].bitcast(F32)
             for g in range(PASSES):
                 for u in range(2):
@@ -119,11 +120,11 @@ def tile_lambdarank_head_gradient_s11_kernel(tc, d_bytes, d_scale, v, delta, ipw
         def d_quantize(j):
             nc.vector.quantize_mx(out=d_codes[j][:].bitcast(E4M3X4), scales=d_planes[j][:], in_=grouped[j][:])
 
-        diff, enc = {}, {}
+        diff, encoded = {}, {}
         sig, h_raw = {}, {}
 
         def score(j):
-            diff[j] = psum.tile([P, RANKERS], F32, name="df")
+            diff[j] = psum.tile([P, RANKERS], F32, name="mm", bufs=4)
             for g in range(PASSES):
                 cols = slice(g * P, (g + 1) * P)
                 nc.tensor.matmul_mx(
@@ -138,11 +139,11 @@ def tile_lambdarank_head_gradient_s11_kernel(tc, d_bytes, d_scale, v, delta, ipw
             nc.scalar.activation(out=sig[s][:, t, :], in_=diff[j][:], func=SIGMOID, scale=-1.0)
 
         def encode(j, half):
-            enc[j, half] = psum.tile([P, 512], F32, name=f"en{half}")
+            encoded[j, half] = psum.tile([P, 512], F32, name="mm", bufs=4)
             for g in range(PASSES):
                 cols = slice(g * P, (g + 1) * P)
                 nc.tensor.matmul_mx(
-                    out=enc[j, half][:], lhsT=d_codes[j][:, cols].bitcast(E4M3X4), lhsT_scale=d_planes[j][:, cols],
+                    out=encoded[j, half][:], lhsT=d_codes[j][:, cols].bitcast(E4M3X4), lhsT_scale=d_planes[j][:, cols],
                     rhs=e_w[g][:, 1024 * half : 1024 * (half + 1)].bitcast(E2M1X4), rhs_scale=e_s[:, g, 512 * half : 512 * (half + 1)],
                     start=(g == 0), stop=(g == PASSES - 1),
                 )
@@ -151,7 +152,7 @@ def tile_lambdarank_head_gradient_s11_kernel(tc, d_bytes, d_scale, v, delta, ipw
             s, t = divmod(j, PACK)
             if t == 0:
                 h_raw[s, half] = work.tile([P, PACK, 512], BF16, name=f"h_raw{half}", bufs=2, align_bytes=64)
-            nc.scalar.activation(out=h_raw[s, half][:, t, :], in_=enc[j, half][:], func=COPY, scale=ipw_f[:, s, t : t + 1])
+            nc.scalar.activation(out=h_raw[s, half][:, t, :], in_=encoded[j, half][:], func=COPY, scale=ipw_f[:, s, t : t + 1])
 
         lam_codes = [keep.tile([P, RANKERS], U32, name=f"lam_codes{s}", align_bytes=64) for s in range(GROUPS)]
         lam_planes = [keep.tile([P, RANKERS], U8, name=f"lam_planes{s}", align_bytes=64) for s in range(GROUPS)]
@@ -175,9 +176,9 @@ def tile_lambdarank_head_gradient_s11_kernel(tc, d_bytes, d_scale, v, delta, ipw
                 out=lam_codes[s][:].bitcast(E4M3X4), scales=lam_planes[s][:], in_=lam[s][:].rearrange("p n t -> p (n t)")
             )
 
-        def h_interleave(s, half):
+        def h_interleave(s, half, copy=nc.vector.tensor_copy):
             h_grp[s, half] = work.tile([P, 512, PACK], BF16, name="h_grp", bufs=2, align_bytes=64)
-            nc.vector.tensor_copy(
+            copy(
                 out=h_grp[s, half][:].rearrange("p (c i) t -> p c t i", i=4),
                 in_=h_raw[s, half][:].rearrange("p t (c i) -> p c t i", i=4),
             )
@@ -189,85 +190,138 @@ def tile_lambdarank_head_gradient_s11_kernel(tc, d_bytes, d_scale, v, delta, ipw
             )
 
         acc = {}
-        late_banks = ("tp", "df", "en0", "en1")
+        banks = {(0, 0): "acc0", (0, 1): "acc1", (0, 2): "tp0", (0, 3): "tp1", (1, 0): "mm", (1, 1): "mm", (1, 2): "mm", (1, 3): "mm"}
 
         def update(s, half, m):
             if s == 0:
-                acc[half, m] = psum.tile([P, 512], F32, name=f"acc{m}" if half == 0 else late_banks[m])
+                acc[half, m] = psum.tile([P, 512], F32, name=banks[half, m], bufs=4 if half == 1 else 1)
             cols = slice(m * P, (m + 1) * P)
             nc.tensor.matmul_mx(
                 out=acc[half, m][:], lhsT=lam_codes[s][:, cols].bitcast(E4M3X4), lhsT_scale=lam_planes[s][:, cols],
-                rhs=h_codes[s, half][:].bitcast(E4M3X4), rhs_scale=h_planes[s, half][:], start=(s == 0), stop=(s == GROUPS - 1),
+                rhs=h_codes[s, half][:].bitcast(E4M3X4), rhs_scale=h_planes[s, half][:], start=(s == 0), stop=(s == GROUPS - 1 - half),
             )
 
         def store(half, m, engine):
-            res = work.tile([P, 512], F32, name="res", bufs=4)
+            res = work.tile([P, 512], F32, name="res", bufs=8)
             if engine == "scalar":
                 nc.scalar.copy(out=res[:], in_=acc[half, m][:])
             else:
                 nc.vector.tensor_copy(out=res[:], in_=acc[half, m][:])
             nc.sync.dma_start(out=out[m * P : (m + 1) * P, 512 * half : 512 * (half + 1)], in_=res[:])
 
-        widen(0)
-        turn(0)
-        gather(0)
-        widen(1)
-        v_interleave(0)
-        nc.vector.tensor_copy(out=ipw_f[:], in_=ipw_bf[:])
-        d_quantize(0)
-        v_interleave(1)
-        v_quantize(0)
-        for j in range(TILES):
-            prev = j // PACK - 1
-            t = j % PACK
-            if j + 2 < TILES:
-                widen(j + 2)
-            if j == 0:
-                v_quantize(1)
-            if j + 1 < TILES:
-                turn(j + 1)
-                gather(j + 1)
+        last = GROUPS - 1
+        pairs = TILES // 2
+        queue = list(range(TILES))
+
+        def widen_next(n):
+            for step in range(n):
+                if queue:
+                    widen(queue.pop(0))
+
+        def enc(j, half):
+            encode(j, half)
+            weigh(j, half)
+
+        def scr(j):
             score(j)
             sigmoid(j)
-            for half in range(HALVES):
-                encode(j, half)
-                weigh(j, half)
-            if prev >= 0:
-                if t == 0:
-                    lam_mult(prev, 0)
-                elif t == 1:
-                    lam_quantize(prev)
-                elif t == 2:
-                    h_quantize(prev, 0)
-                else:
-                    h_quantize(prev, 1)
-                    for m in range(QTILES):
-                        update(prev, 0, m)
-            if j + 1 < TILES:
-                d_quantize(j + 1)
-            if prev >= 0:
-                if t == 0:
-                    lam_mult(prev, 1)
-                elif t == 1:
-                    h_interleave(prev, 0)
-                elif t == 2:
+
+        v_interleave(0, 0, 1, nc.vector.tensor_copy)
+        widen_next(1)
+        turn(0)
+        gather(0)
+        widen_next(1)
+        turn(1)
+        d_quantize(0)
+        gather(1)
+        v_interleave(1, 0, 2, nc.scalar.copy)
+        v_quantize(0)
+        nc.vector.tensor_copy(out=ipw_f[:], in_=ipw_bf[:])
+        widen_next(1)
+        d_quantize(1)
+        widen_next(1)
+        ahead = (2, 2, 1, 2, 1, 2, 1, 1)
+        for p in range(pairs):
+            grp, odd = divmod(p, 2)
+            prev = grp - 1
+            a, b = 2 * p, 2 * p + 1
+            nxt = [j for j in (2 * p + 2, 2 * p + 3) if j < TILES]
+            for j in nxt:
+                turn(j)
+                gather(j)
+                if j == 2:
+                    v_interleave(1, 1, 2, nc.scalar.copy)
+            if p == 0:
+                enc(a, 0)
+                enc(a, 1)
+                enc(b, 0)
+                enc(b, 1)
+            elif p == 1:
+                scr(a - 2)
+                scr(b - 2)
+                scr(a)
+                scr(b)
+                enc(a, 0)
+                enc(a, 1)
+                enc(b, 0)
+                enc(b, 1)
+            else:
+                scr(a)
+                scr(b)
+                enc(a, 0)
+                enc(b, 0)
+                enc(a, 1)
+                enc(b, 1)
+            k = ahead[p]
+            if prev < 0:
+                widen_next(1)
+                if nxt: d_quantize(nxt[0])
+                widen_next(1)
+                if nxt: d_quantize(nxt[1])
+                widen_next(k)
+                if p == 0: v_quantize(1)
+            elif odd == 0:
+                lam_mult(prev, 0)
+                if nxt: d_quantize(nxt[0])
+                lam_mult(prev, 1)
+                if nxt: d_quantize(nxt[1])
+                h_interleave(prev, 0)
+                lam_quantize(prev)
+                widen_next(k)
+                h_quantize(prev, 0)
+            else:
+                if p < pairs - 1:
                     h_interleave(prev, 1)
-        last = GROUPS - 1
-        for m in range(QTILES):
+                widen_next(1)
+                if nxt: d_quantize(nxt[0])
+                widen_next(1)
+                if nxt: d_quantize(nxt[1])
+                if p < pairs - 1:
+                    h_quantize(prev, 1)
+                widen_next(k - 2)
+                for m in range(2):
+                    update(prev, 0, m)
+        for m in range(2, QTILES):
             for s in range(last):
+                update(s, 0, m)
+        for m in range(QTILES):
+            for s in range(last - 1):
                 update(s, 1, m)
         lam_mult(last, 0)
         lam_mult(last, 1)
         h_interleave(last, 0)
+        h_interleave(last, 1, nc.scalar.copy)
         lam_quantize(last)
-        h_interleave(last, 1)
         h_quantize(last, 0)
         for m in range(QTILES):
             update(last, 0, m)
-        h_quantize(last, 1)
-        for m in range(QTILES):
-            update(last, 1, m)
         for m in range(QTILES):
             store(0, m, "scalar")
+        h_interleave(last - 1, 1)
+        h_quantize(last, 1)
+        h_quantize(last - 1, 1)
+        for s in (last, last - 1):
+            for m in range(QTILES):
+                update(s, 1, m)
         for m in range(QTILES):
-            store(1, m, "vector" if m % 2 == 0 else "scalar")
+            store(1, m, "scalar" if m % 2 == 0 else "vector")

@@ -40,6 +40,7 @@ def tile_lambdarank_head_gradient_s11_kernel(tc, d_bytes, d_scale, v, delta, ipw
 
         ctx.enter_context(tc.manual_schedule())
 
+        scale_kp = keep.tile([P, PASSES, PACK], F32, name="scale_kp")
         scale_bc = keep.tile([P, RAW], F32, name="scale_bc", align_bytes=64)
         raw = [keep.tile([P, PACK, RAW], U8, name=f"raw{s}", align_bytes=64) for s in range(GROUPS)]
         dlt = [keep.tile([P, PACK, RANKERS], BF16, name=f"dlt{s}", align_bytes=64) for s in range(GROUPS)]
@@ -60,17 +61,18 @@ def tile_lambdarank_head_gradient_s11_kernel(tc, d_bytes, d_scale, v, delta, ipw
         v_view = v.rearrange("(g p t) n -> g p t n", p=P, t=PACK)
         s_view = e_scales.rearrange("g r n -> r g n")
 
-        nc.sync.dma_start(out=v_raw[0][:], in_=v_view[0])
-        nc.scalar.dma_start(out=scale_bc[:], in_=d_scale.rearrange("o k -> (o k)").partition_broadcast(P))
-        nc.sync.dma_start(out=raw[0][:, 0, :], in_=d_view[0][:, 0, :])
-        nc.sync.dma_start(out=raw[0][:, 1:, :], in_=d_view[0][:, 1:, :])
+        nc.scalar.dma_start(out=scale_kp[:], in_=d_scale.rearrange("o (g p t) -> p (o g) t", p=P, t=PACK))
+        nc.scalar.dma_start(out=ipw_bf[:], in_=ipw.rearrange("(s m t) -> m s t", m=P, t=PACK))
+        nc.sync.dma_start(out=raw[0][:, 0:1, :], in_=d_view[0][:, 0:1, :])
+        nc.sync.dma_start(out=raw[0][:, 1:4, :], in_=d_view[0][:, 1:4, :])
         for g in range(PASSES):
             nc.sync.dma_start(out=e_w[g][:], in_=e_words[g])
         for quad in range(4):
             nc.sync.dma_start(out=e_s[32 * quad : 32 * quad + 4].bitcast(I32), in_=s_view[4 * quad : 4 * quad + 4].bitcast(I32))
-        nc.sync.dma_start(out=ipw_bf[:], in_=ipw.rearrange("(s m t) -> m s t", m=P, t=PACK))
-        nc.sync.dma_start(out=v_raw[1][:], in_=v_view[1])
+        nc.sync.dma_start(out=v_raw[0][:], in_=v_view[0])
+        nc.sync.dma_start(out=scale_bc[:], in_=d_scale.rearrange("o k -> (o k)").partition_broadcast(P))
         nc.sync.dma_start(out=raw[1][:], in_=d_view[1])
+        nc.sync.dma_start(out=v_raw[1][:], in_=v_view[1])
         nc.sync.dma_start(out=raw[2][:], in_=d_view[2])
         nc.sync.dma_start(out=dlt[0][:], in_=dlt_view[0])
         nc.sync.dma_start(out=raw[3][:], in_=d_view[3])
@@ -102,6 +104,20 @@ def tile_lambdarank_head_gradient_s11_kernel(tc, d_bytes, d_scale, v, delta, ipw
             nc.vector.tensor_tensor(
                 out=scaled[j][:], in0=raw[j // PACK][:, j % PACK, :].bitcast(FP8), in1=scale_bc[:], op=MULT
             )
+
+        def widen_only(j, copy):
+            scaled[j] = work.tile([P, RAW], BF16, name="scaled", bufs=9, align_bytes=64)
+            copy(out=scaled[j][:], in_=raw[j // PACK][:, j % PACK, :].bitcast(FP8))
+
+        def scale_turned(j):
+            grouped[j] = work.tile([P, PASSES * P * PACK], BF16, name="grouped", align_bytes=64)
+            for g in range(PASSES):
+                nc.vector.tensor_tensor(
+                    out=grouped[j][:, 512 * g : 512 * (g + 1)].rearrange("p (r u e) -> p r u e", u=2, e=2),
+                    in0=turned[j][:, g].bitcast(BF16).rearrange("p u (r e) -> p r u e", e=2),
+                    in1=scale_kp[:, g : g + 1, :].rearrange("p o (u e) -> p o u e", e=2).to_broadcast([P, P, 2, 2]),
+                    op=MULT,
+                )
 
         def turn(j):
             turned[j] = psum.tile([P, PASSES, 2, P], F32, name=f"tp{j % 2}")
@@ -211,7 +227,7 @@ def tile_lambdarank_head_gradient_s11_kernel(tc, d_bytes, d_scale, v, delta, ipw
 
         last = GROUPS - 1
         pairs = TILES // 2
-        queue = list(range(TILES))
+        queue = list(range(PACK, TILES))
 
         def widen_next(n):
             for step in range(n):
@@ -226,20 +242,18 @@ def tile_lambdarank_head_gradient_s11_kernel(tc, d_bytes, d_scale, v, delta, ipw
             score(j)
             sigmoid(j)
 
-        v_interleave(0, 0, 1, nc.vector.tensor_copy)
-        widen_next(1)
+        widen_only(0, nc.vector.tensor_copy)
         turn(0)
-        gather(0)
-        widen_next(1)
-        turn(1)
-        d_quantize(0)
-        gather(1)
-        v_interleave(1, 0, 2, nc.scalar.copy)
-        v_quantize(0)
         nc.vector.tensor_copy(out=ipw_f[:], in_=ipw_bf[:])
-        widen_next(1)
+        for j in range(1, PACK):
+            widen_only(j, nc.scalar.copy)
+        turn(1)
+        scale_turned(0)
+        scale_turned(1)
+        d_quantize(0)
         d_quantize(1)
-        widen_next(1)
+        for part in range(2):
+            v_interleave(0, part, 2, nc.scalar.copy)
         ahead = (2, 2, 1, 2, 1, 2, 1, 1)
         for p in range(pairs):
             grp, odd = divmod(p, 2)
@@ -248,14 +262,17 @@ def tile_lambdarank_head_gradient_s11_kernel(tc, d_bytes, d_scale, v, delta, ipw
             nxt = [j for j in (2 * p + 2, 2 * p + 3) if j < TILES]
             for j in nxt:
                 turn(j)
-                gather(j)
-                if j == 2:
-                    v_interleave(1, 1, 2, nc.scalar.copy)
+                if j < PACK:
+                    scale_turned(j)
+                else:
+                    gather(j)
             if p == 0:
                 enc(a, 0)
                 enc(a, 1)
+                v_interleave(1, 0, 2, nc.scalar.copy)
                 enc(b, 0)
                 enc(b, 1)
+                v_interleave(1, 1, 2, nc.scalar.copy)
             elif p == 1:
                 scr(a - 2)
                 scr(b - 2)
@@ -279,7 +296,9 @@ def tile_lambdarank_head_gradient_s11_kernel(tc, d_bytes, d_scale, v, delta, ipw
                 widen_next(1)
                 if nxt: d_quantize(nxt[1])
                 widen_next(k)
-                if p == 0: v_quantize(1)
+                if p == 0:
+                    v_quantize(0)
+                    v_quantize(1)
             elif odd == 0:
                 lam_mult(prev, 0)
                 if nxt: d_quantize(nxt[0])
@@ -317,8 +336,8 @@ def tile_lambdarank_head_gradient_s11_kernel(tc, d_bytes, d_scale, v, delta, ipw
             update(last, 0, m)
         for m in range(QTILES):
             store(0, m, "scalar")
-        h_interleave(last - 1, 1)
         h_quantize(last, 1)
+        h_interleave(last - 1, 1)
         h_quantize(last - 1, 1)
         for s in (last, last - 1):
             for m in range(QTILES):

@@ -25,6 +25,8 @@ HALVES = FEATS // 512
 TILES = PAIRS // P
 QTILES = RANKERS // P
 
+PROGRAM = """c0 T0 C1 C2 C3 v T1 p0 v x d T2 e p1 p2 d T3 p3 w q w d e w v v t e w q e d e t d w e w t s s e s w t e d d e s i00 w t d h00 l00 d t w e e s d e w i01 l01 t t w s e s h01 L0 w s s e e e e e d t d d t i10 i11 u001 e e l10 s e h10 s l11 d e s t t u000 e e u003 e L1 i20 e d h20 s u100 u103 l20 s d e u101 s l21 e s e h11 e e i21 L2 e u113 u203 h21 u110 I31 u012 l30 i30 L30 u213 l32 u202 u013 u201 h30 u211 L32 u212 u200 l31 u102 u210 h31 u002 L31 l33 u300 u302 u010 u011 o00 u310 o02 u111 u311 u312 o10 u301 L33 u313 O11 O01 u112 o13 O12 u303 O03"""
+
 FLOPS = 2 * PAIRS * RAW * RANKERS + 2 * PAIRS * RAW * FEATS + 2 * RANKERS * PAIRS * FEATS
 
 
@@ -151,7 +153,7 @@ def tile_lambdarank_head_gradient_s11_kernel(tc, d_bytes, d_scale, v, delta, ipw
         def sigmoid(j):
             s, t = divmod(j, PACK)
             if t == 0:
-                sig[s] = work.tile([P, PACK, RANKERS], F32, name="sig", bufs=2, align_bytes=64)
+                sig[s] = work.tile([P, PACK, RANKERS], F32, name="sig", bufs=3, align_bytes=64)
             nc.scalar.activation(out=sig[s][:, t, :], in_=diff[j][:], func=SIGMOID, scale=-1.0)
 
         def encode(j, half):
@@ -176,10 +178,10 @@ def tile_lambdarank_head_gradient_s11_kernel(tc, d_bytes, d_scale, v, delta, ipw
         h_planes = {(s, h): keep.tile([P, 512], U8, name=f"h_planes{s}_{h}", align_bytes=64) for s in range(GROUPS) for h in range(HALVES)}
         lam, h_grp = {}, {}
 
-        def lam_mult(s, part):
+        def lam_mult(s, part, parts):
             if part == 0:
                 lam[s] = work.tile([P, RANKERS, PACK], BF16, name="lam", bufs=2, align_bytes=64)
-            cols = slice(256 * part, 256 * (part + 1))
+            cols = slice(RANKERS // parts * part, RANKERS // parts * (part + 1))
             nc.vector.tensor_tensor(
                 out=lam[s][:, cols, :].rearrange("p (c i) t -> p c t i", i=4),
                 in0=sig[s][:, :, cols].rearrange("p t (c i) -> p c t i", i=4),
@@ -187,13 +189,15 @@ def tile_lambdarank_head_gradient_s11_kernel(tc, d_bytes, d_scale, v, delta, ipw
                 op=MULT,
             )
 
-        def lam_quantize(s):
+        def lam_quantize(s, part, parts):
+            cols = slice(RANKERS // parts * part, RANKERS // parts * (part + 1))
             nc.vector.quantize_mx(
-                out=lam_codes[s][:].bitcast(E4M3X4), scales=lam_planes[s][:], in_=lam[s][:].rearrange("p n t -> p (n t)")
+                out=lam_codes[s][:, cols].bitcast(E4M3X4), scales=lam_planes[s][:, cols],
+                in_=lam[s][:, cols, :].rearrange("p n t -> p (n t)"),
             )
 
         def h_interleave(s, half, copy=nc.vector.tensor_copy):
-            h_grp[s, half] = work.tile([P, 512, PACK], BF16, name="h_grp", bufs=2, align_bytes=64)
+            h_grp[s, half] = work.tile([P, 512, PACK], BF16, name="h_grp", bufs=4, align_bytes=64)
             copy(
                 out=h_grp[s, half][:].rearrange("p (c i) t -> p c t i", i=4),
                 in_=h_raw[s, half][:].rearrange("p t (c i) -> p c t i", i=4),
@@ -205,19 +209,21 @@ def tile_lambdarank_head_gradient_s11_kernel(tc, d_bytes, d_scale, v, delta, ipw
                 in_=h_grp[s, half][:].rearrange("p n t -> p (n t)"),
             )
 
-        acc = {}
+        acc, summed = {}, {}
         banks = {(0, 0): "acc0", (0, 1): "acc1", (0, 2): "tp0", (0, 3): "tp1", (1, 0): "mm", (1, 1): "mm", (1, 2): "mm", (1, 3): "mm"}
 
         def update(s, half, m):
-            if s == 0:
+            summed[half, m] = summed.get((half, m), 0) + 1
+            if summed[half, m] == 1:
                 acc[half, m] = psum.tile([P, 512], F32, name=banks[half, m], bufs=4 if half == 1 else 1)
             cols = slice(m * P, (m + 1) * P)
             nc.tensor.matmul_mx(
                 out=acc[half, m][:], lhsT=lam_codes[s][:, cols].bitcast(E4M3X4), lhsT_scale=lam_planes[s][:, cols],
-                rhs=h_codes[s, half][:].bitcast(E4M3X4), rhs_scale=h_planes[s, half][:], start=(s == 0), stop=(s == GROUPS - 1 - half),
+                rhs=h_codes[s, half][:].bitcast(E4M3X4), rhs_scale=h_planes[s, half][:], start=(summed[half, m] == 1), stop=(summed[half, m] == GROUPS),
             )
 
         def store(half, m, engine):
+            assert summed[half, m] == GROUPS
             res = work.tile([P, 512], F32, name="res", bufs=8)
             if engine == "scalar":
                 nc.scalar.copy(out=res[:], in_=acc[half, m][:])
@@ -226,121 +232,56 @@ def tile_lambdarank_head_gradient_s11_kernel(tc, d_bytes, d_scale, v, delta, ipw
             nc.sync.dma_start(out=out[m * P : (m + 1) * P, 512 * half : 512 * (half + 1)], in_=res[:])
 
         last = GROUPS - 1
-        pairs = TILES // 2
-        queue = list(range(PACK, TILES))
+        order = dict(w=list(range(PACK, TILES)), t=list(range(PACK, TILES)), d=list(range(TILES)), s=list(range(TILES)),
+                     e=[(j, h) for j in range(TILES) for h in range(HALVES)], v=[(g, part) for g in range(PASSES) for part in range(2)],
+                     q=list(range(PASSES)))
 
-        def widen_next(n):
-            for step in range(n):
-                if queue:
-                    widen(queue.pop(0))
+        def step(token):
+            kind, arg = token[0], [int(x) for x in token[1:]]
+            nxt = order[kind].pop(0) if kind in order else None
+            if kind == "w":
+                widen(nxt)
+            elif kind == "t":
+                turn(nxt)
+                gather(nxt)
+            elif kind == "d":
+                d_quantize(nxt)
+            elif kind == "s":
+                score(nxt)
+                sigmoid(nxt)
+            elif kind == "e":
+                encode(*nxt)
+                weigh(*nxt)
+            elif kind == "v":
+                v_interleave(*nxt, 2, nc.scalar.copy)
+            elif kind == "q":
+                v_quantize(nxt)
+            elif kind == "c":
+                widen_only(arg[0], nc.vector.tensor_copy)
+            elif kind == "C":
+                widen_only(arg[0], nc.scalar.copy)
+            elif kind == "T":
+                turn(arg[0])
+            elif kind == "p":
+                scale_turned(arg[0])
+            elif kind == "l":
+                lam_mult(arg[0], arg[1], 4 if arg[0] == last else 2)
+            elif kind == "L":
+                lam_quantize(arg[0], arg[1] if arg[0] == last else 0, 4 if arg[0] == last else 1)
+            elif kind == "i":
+                h_interleave(*arg)
+            elif kind == "I":
+                h_interleave(*arg, nc.scalar.copy)
+            elif kind == "h":
+                h_quantize(*arg)
+            elif kind == "u":
+                update(*arg)
+            elif kind == "x":
+                nc.vector.tensor_copy(out=ipw_f[:], in_=ipw_bf[:])
+            elif kind == "o":
+                store(arg[0], arg[1], "scalar")
+            elif kind == "O":
+                store(arg[0], arg[1], "vector")
 
-        def enc(j, half):
-            encode(j, half)
-            weigh(j, half)
-
-        def scr(j):
-            score(j)
-            sigmoid(j)
-
-        widen_only(0, nc.vector.tensor_copy)
-        turn(0)
-        nc.vector.tensor_copy(out=ipw_f[:], in_=ipw_bf[:])
-        for j in range(1, PACK):
-            widen_only(j, nc.scalar.copy)
-        turn(1)
-        scale_turned(0)
-        scale_turned(1)
-        d_quantize(0)
-        d_quantize(1)
-        for part in range(2):
-            v_interleave(0, part, 2, nc.scalar.copy)
-        ahead = (2, 2, 1, 2, 1, 2, 1, 1)
-        for p in range(pairs):
-            grp, odd = divmod(p, 2)
-            prev = grp - 1
-            a, b = 2 * p, 2 * p + 1
-            nxt = [j for j in (2 * p + 2, 2 * p + 3) if j < TILES]
-            for j in nxt:
-                turn(j)
-                if j < PACK:
-                    scale_turned(j)
-                else:
-                    gather(j)
-            if p == 0:
-                enc(a, 0)
-                enc(a, 1)
-                v_interleave(1, 0, 2, nc.scalar.copy)
-                enc(b, 0)
-                enc(b, 1)
-                v_interleave(1, 1, 2, nc.scalar.copy)
-            elif p == 1:
-                scr(a - 2)
-                scr(b - 2)
-                scr(a)
-                scr(b)
-                enc(a, 0)
-                enc(a, 1)
-                enc(b, 0)
-                enc(b, 1)
-            else:
-                scr(a)
-                scr(b)
-                enc(a, 0)
-                enc(b, 0)
-                enc(a, 1)
-                enc(b, 1)
-            k = ahead[p]
-            if prev < 0:
-                widen_next(1)
-                if nxt: d_quantize(nxt[0])
-                widen_next(1)
-                if nxt: d_quantize(nxt[1])
-                widen_next(k)
-                if p == 0:
-                    v_quantize(0)
-                    v_quantize(1)
-            elif odd == 0:
-                lam_mult(prev, 0)
-                if nxt: d_quantize(nxt[0])
-                lam_mult(prev, 1)
-                if nxt: d_quantize(nxt[1])
-                h_interleave(prev, 0)
-                lam_quantize(prev)
-                widen_next(k)
-                h_quantize(prev, 0)
-            else:
-                if p < pairs - 1:
-                    h_interleave(prev, 1)
-                widen_next(1)
-                if nxt: d_quantize(nxt[0])
-                widen_next(1)
-                if nxt: d_quantize(nxt[1])
-                if p < pairs - 1:
-                    h_quantize(prev, 1)
-                widen_next(k - 2)
-                for m in range(2):
-                    update(prev, 0, m)
-        for m in range(2, QTILES):
-            for s in range(last):
-                update(s, 0, m)
-        for m in range(QTILES):
-            for s in range(last - 1):
-                update(s, 1, m)
-        lam_mult(last, 0)
-        lam_mult(last, 1)
-        h_interleave(last, 0)
-        h_interleave(last, 1, nc.scalar.copy)
-        lam_quantize(last)
-        h_quantize(last, 0)
-        for m in range(QTILES):
-            update(last, 0, m)
-        for m in range(QTILES):
-            store(0, m, "scalar")
-        h_quantize(last, 1)
-        h_interleave(last - 1, 1)
-        h_quantize(last - 1, 1)
-        for s in (last, last - 1):
-            for m in range(QTILES):
-                update(s, 1, m)
-        for m in range(QTILES):
-            store(1, m, "scalar" if m % 2 == 0 else "vector")
+        for token in PROGRAM.split():
+            step(token)

from contextlib import ExitStack

import concourse.mybir as mybir
from concourse.masks import make_identity

F32 = mybir.dt.float32
BF16 = mybir.dt.bfloat16
I32 = mybir.dt.int32
U32 = mybir.dt.uint32
U8 = mybir.dt.uint8
FP8 = mybir.dt.float8_e4m3fn
E4M3X4 = mybir.dt.float8_e4m3fn_x4
E2M1X4 = mybir.dt.float4_e2m1fn_x4
MULT = mybir.AluOpType.mult
COPY = mybir.ActivationFunctionType.Copy
SIGMOID = mybir.ActivationFunctionType.Sigmoid

PAIRS, RAW, RANKERS, FEATS = 2048, 1024, 512, 1024
P = 128
PACK = 4
GROUP = P * PACK
GROUPS = PAIRS // GROUP
PASSES = RAW // GROUP
HALVES = FEATS // 512
TILES = PAIRS // P
QTILES = RANKERS // P

PROGRAM = """c0 T0 C1 C2 C3 v T1 p0 v x d T2 e p1 p2 d T3 p3 w q w d e w v v t e w q e d e t d w e w t s s e s w t e d d e s i00 w t d h00 l00 d t w e e s d e w i01 l01 t t w s e s h01 L0 w s s e e e e e d t d d t i10 i11 u001 e e l10 s e h10 s l11 d e s t t u000 e e u003 e L1 i20 e d h20 s u100 u103 l20 s d e u101 s l21 e s e h11 e e i21 L2 e u113 u203 h21 u110 I31 u012 l30 i30 L30 u213 l32 u202 u013 u201 h30 u211 L32 u212 u200 l31 u102 u210 h31 u002 L31 l33 u300 u302 u010 u011 o00 u310 o02 u111 u311 u312 o10 u301 L33 u313 O11 O01 u112 o13 O12 u303 O03"""

FLOPS = 2 * PAIRS * RAW * RANKERS + 2 * PAIRS * RAW * FEATS + 2 * RANKERS * PAIRS * FEATS


def tile_lambdarank_head_gradient_s11_kernel(tc, d_bytes, d_scale, v, delta, ipw, e_words, e_scales, out):
    nc = tc.nc
    with ExitStack() as ctx:
        keep = ctx.enter_context(tc.tile_pool(name="keep", bufs=1))
        work = ctx.enter_context(tc.tile_pool(name="work", bufs=3))
        psum = ctx.enter_context(tc.psum_pool(name="psum", bufs=1))

        ident = keep.tile([P, P], F32, name="ident")
        make_identity(nc, ident[:])

        ctx.enter_context(tc.manual_schedule())

        scale_kp = keep.tile([P, PASSES, PACK], F32, name="scale_kp")
        scale_bc = keep.tile([P, RAW], F32, name="scale_bc", align_bytes=64)
        raw = [keep.tile([P, PACK, RAW], U8, name=f"raw{s}", align_bytes=64) for s in range(GROUPS)]
        dlt = [keep.tile([P, PACK, RANKERS], BF16, name=f"dlt{s}", align_bytes=64) for s in range(GROUPS)]
        v_raw = [keep.tile([P, PACK, RANKERS], BF16, name=f"v_raw{g}", align_bytes=64) for g in range(PASSES)]
        e_w = [keep.tile([P, 2 * FEATS], U8, name=f"e_w{g}", align_bytes=64) for g in range(PASSES)]
        e_s = keep.tile([P, PASSES, FEATS], U8, name="e_s", align_bytes=64)
        ipw_bf = keep.tile([P, GROUPS, PACK], BF16, name="ipw_bf")
        ipw_f = keep.tile([P, GROUPS, PACK], F32, name="ipw_f")

        warm = keep.tile([P, 1], F32, name="warm")
        nc.vector.memset(warm[:], 0.0)
        warm_out = keep.tile([P, 1], F32, name="warm_out")
        nc.scalar.activation(out=warm_out[:], in_=warm[:], func=SIGMOID, scale=-1.0)
        nc.vector.memset(e_s[:].bitcast(I32), 0)

        d_view = d_bytes.rearrange("(s m t) k -> s m t k", m=P, t=PACK)
        dlt_view = delta.rearrange("(s m t) q -> s m t q", m=P, t=PACK)
        v_view = v.rearrange("(g p t) n -> g p t n", p=P, t=PACK)
        s_view = e_scales.rearrange("g r n -> r g n")

        nc.scalar.dma_start(out=scale_kp[:], in_=d_scale.rearrange("o (g p t) -> p (o g) t", p=P, t=PACK))
        nc.scalar.dma_start(out=ipw_bf[:], in_=ipw.rearrange("(s m t) -> m s t", m=P, t=PACK))
        nc.sync.dma_start(out=raw[0][:, 0:1, :], in_=d_view[0][:, 0:1, :])
        nc.sync.dma_start(out=raw[0][:, 1:4, :], in_=d_view[0][:, 1:4, :])
        for g in range(PASSES):
            nc.sync.dma_start(out=e_w[g][:], in_=e_words[g])
        for quad in range(4):
            nc.sync.dma_start(out=e_s[32 * quad : 32 * quad + 4].bitcast(I32), in_=s_view[4 * quad : 4 * quad + 4].bitcast(I32))
        nc.sync.dma_start(out=v_raw[0][:], in_=v_view[0])
        nc.sync.dma_start(out=scale_bc[:], in_=d_scale.rearrange("o k -> (o k)").partition_broadcast(P))
        nc.sync.dma_start(out=raw[1][:], in_=d_view[1])
        nc.sync.dma_start(out=v_raw[1][:], in_=v_view[1])
        nc.sync.dma_start(out=raw[2][:], in_=d_view[2])
        nc.sync.dma_start(out=dlt[0][:], in_=dlt_view[0])
        nc.sync.dma_start(out=raw[3][:], in_=d_view[3])
        for s in range(1, GROUPS):
            nc.sync.dma_start(out=dlt[s][:], in_=dlt_view[s])

        v_codes = [keep.tile([P, RANKERS], U32, name=f"v_codes{g}", align_bytes=64) for g in range(PASSES)]
        v_planes = [keep.tile([P, RANKERS], U8, name=f"v_planes{g}", align_bytes=64) for g in range(PASSES)]
        v_grp = [keep.tile([P, RANKERS, PACK], BF16, name=f"v_grp{g}", align_bytes=64) for g in range(PASSES)]

        def v_interleave(g, part, parts, copy):
            cols = slice(RANKERS // parts * part, RANKERS // parts * (part + 1))
            copy(
                out=v_grp[g][:, cols, :].rearrange("p (c i) t -> p c t i", i=4),
                in_=v_raw[g][:, :, cols].rearrange("p t (c i) -> p c t i", i=4),
            )

        def v_quantize(g):
            nc.vector.quantize_mx(
                out=v_codes[g][:].bitcast(E4M3X4), scales=v_planes[g][:], in_=v_grp[g][:].rearrange("p n t -> p (n t)")
            )

        d_codes = [keep.tile([P, PASSES * P], U32, name=f"d_codes{j}", align_bytes=64) for j in range(TILES)]
        d_planes = [keep.tile([P, PASSES * P], U8, name=f"d_planes{j}", align_bytes=64) for j in range(TILES)]
        scaled, turned, grouped = {}, {}, {}

        def widen(j):
            scaled[j] = work.tile([P, RAW], BF16, name="scaled", bufs=9, align_bytes=64)
            nc.vector.tensor_tensor(
                out=scaled[j][:], in0=raw[j // PACK][:, j % PACK, :].bitcast(FP8), in1=scale_bc[:], op=MULT
            )

        def widen_only(j, copy):
            scaled[j] = work.tile([P, RAW], BF16, name="scaled", bufs=9, align_bytes=64)
            copy(out=scaled[j][:], in_=raw[j // PACK][:, j % PACK, :].bitcast(FP8))

        def scale_turned(j):
            grouped[j] = work.tile([P, PASSES * P * PACK], BF16, name="grouped", align_bytes=64)
            for g in range(PASSES):
                nc.vector.tensor_tensor(
                    out=grouped[j][:, 512 * g : 512 * (g + 1)].rearrange("p (r u e) -> p r u e", u=2, e=2),
                    in0=turned[j][:, g].bitcast(BF16).rearrange("p u (r e) -> p r u e", e=2),
                    in1=scale_kp[:, g : g + 1, :].rearrange("p o (u e) -> p o u e", e=2).to_broadcast([P, P, 2, 2]),
                    op=MULT,
                )

        def turn(j):
            turned[j] = psum.tile([P, PASSES, 2, P], F32, name=f"tp{j % 2}")
            words = scaled[j][:].bitcast(F32)
            for g in range(PASSES):
                for u in range(2):
                    nc.tensor.transpose(turned[j][:, g, u, :], words[:, 256 * g + u : 256 * (g + 1) : 2], ident[:])

        def gather(j):
            grouped[j] = work.tile([P, PASSES * P * PACK], BF16, name="grouped", align_bytes=64)
            nc.scalar.copy(
                out=grouped[j][:].bitcast(F32).rearrange("p (g r u) -> p g r u", g=PASSES, u=2),
                in_=turned[j][:].rearrange("p g u r -> p g r u"),
            )

        def d_quantize(j):
            nc.vector.quantize_mx(out=d_codes[j][:].bitcast(E4M3X4), scales=d_planes[j][:], in_=grouped[j][:])

        diff, encoded = {}, {}
        sig, h_raw = {}, {}

        def score(j):
            diff[j] = psum.tile([P, RANKERS], F32, name="mm", bufs=4)
            for g in range(PASSES):
                cols = slice(g * P, (g + 1) * P)
                nc.tensor.matmul_mx(
                    out=diff[j][:], lhsT=d_codes[j][:, cols].bitcast(E4M3X4), lhsT_scale=d_planes[j][:, cols],
                    rhs=v_codes[g][:].bitcast(E4M3X4), rhs_scale=v_planes[g][:], start=(g == 0), stop=(g == PASSES - 1),
                )

        def sigmoid(j):
            s, t = divmod(j, PACK)
            if t == 0:
                sig[s] = work.tile([P, PACK, RANKERS], F32, name="sig", bufs=3, align_bytes=64)
            nc.scalar.activation(out=sig[s][:, t, :], in_=diff[j][:], func=SIGMOID, scale=-1.0)

        def encode(j, half):
            encoded[j, half] = psum.tile([P, 512], F32, name="mm", bufs=4)
            for g in range(PASSES):
                cols = slice(g * P, (g + 1) * P)
                nc.tensor.matmul_mx(
                    out=encoded[j, half][:], lhsT=d_codes[j][:, cols].bitcast(E4M3X4), lhsT_scale=d_planes[j][:, cols],
                    rhs=e_w[g][:, 1024 * half : 1024 * (half + 1)].bitcast(E2M1X4), rhs_scale=e_s[:, g, 512 * half : 512 * (half + 1)],
                    start=(g == 0), stop=(g == PASSES - 1),
                )

        def weigh(j, half):
            s, t = divmod(j, PACK)
            if t == 0:
                h_raw[s, half] = work.tile([P, PACK, 512], BF16, name=f"h_raw{half}", bufs=2, align_bytes=64)
            nc.scalar.activation(out=h_raw[s, half][:, t, :], in_=encoded[j, half][:], func=COPY, scale=ipw_f[:, s, t : t + 1])

        lam_codes = [keep.tile([P, RANKERS], U32, name=f"lam_codes{s}", align_bytes=64) for s in range(GROUPS)]
        lam_planes = [keep.tile([P, RANKERS], U8, name=f"lam_planes{s}", align_bytes=64) for s in range(GROUPS)]
        h_codes = {(s, h): keep.tile([P, 512], U32, name=f"h_codes{s}_{h}", align_bytes=64) for s in range(GROUPS) for h in range(HALVES)}
        h_planes = {(s, h): keep.tile([P, 512], U8, name=f"h_planes{s}_{h}", align_bytes=64) for s in range(GROUPS) for h in range(HALVES)}
        lam, h_grp = {}, {}

        def lam_mult(s, part, parts):
            if part == 0:
                lam[s] = work.tile([P, RANKERS, PACK], BF16, name="lam", bufs=2, align_bytes=64)
            cols = slice(RANKERS // parts * part, RANKERS // parts * (part + 1))
            nc.vector.tensor_tensor(
                out=lam[s][:, cols, :].rearrange("p (c i) t -> p c t i", i=4),
                in0=sig[s][:, :, cols].rearrange("p t (c i) -> p c t i", i=4),
                in1=dlt[s][:, :, cols].rearrange("p t (c i) -> p c t i", i=4),
                op=MULT,
            )

        def lam_quantize(s, part, parts):
            cols = slice(RANKERS // parts * part, RANKERS // parts * (part + 1))
            nc.vector.quantize_mx(
                out=lam_codes[s][:, cols].bitcast(E4M3X4), scales=lam_planes[s][:, cols],
                in_=lam[s][:, cols, :].rearrange("p n t -> p (n t)"),
            )

        def h_interleave(s, half, copy=nc.vector.tensor_copy):
            h_grp[s, half] = work.tile([P, 512, PACK], BF16, name="h_grp", bufs=4, align_bytes=64)
            copy(
                out=h_grp[s, half][:].rearrange("p (c i) t -> p c t i", i=4),
                in_=h_raw[s, half][:].rearrange("p t (c i) -> p c t i", i=4),
            )

        def h_quantize(s, half):
            nc.vector.quantize_mx(
                out=h_codes[s, half][:].bitcast(E4M3X4), scales=h_planes[s, half][:],
                in_=h_grp[s, half][:].rearrange("p n t -> p (n t)"),
            )

        acc, summed = {}, {}
        banks = {(0, 0): "acc0", (0, 1): "acc1", (0, 2): "tp0", (0, 3): "tp1", (1, 0): "mm", (1, 1): "mm", (1, 2): "mm", (1, 3): "mm"}

        def update(s, half, m):
            summed[half, m] = summed.get((half, m), 0) + 1
            if summed[half, m] == 1:
                acc[half, m] = psum.tile([P, 512], F32, name=banks[half, m], bufs=4 if half == 1 else 1)
            cols = slice(m * P, (m + 1) * P)
            nc.tensor.matmul_mx(
                out=acc[half, m][:], lhsT=lam_codes[s][:, cols].bitcast(E4M3X4), lhsT_scale=lam_planes[s][:, cols],
                rhs=h_codes[s, half][:].bitcast(E4M3X4), rhs_scale=h_planes[s, half][:], start=(summed[half, m] == 1), stop=(summed[half, m] == GROUPS),
            )

        def store(half, m, engine):
            assert summed[half, m] == GROUPS
            res = work.tile([P, 512], F32, name="res", bufs=8)
            if engine == "scalar":
                nc.scalar.copy(out=res[:], in_=acc[half, m][:])
            else:
                nc.vector.tensor_copy(out=res[:], in_=acc[half, m][:])
            nc.sync.dma_start(out=out[m * P : (m + 1) * P, 512 * half : 512 * (half + 1)], in_=res[:])

        last = GROUPS - 1
        order = dict(w=list(range(PACK, TILES)), t=list(range(PACK, TILES)), d=list(range(TILES)), s=list(range(TILES)),
                     e=[(j, h) for j in range(TILES) for h in range(HALVES)], v=[(g, part) for g in range(PASSES) for part in range(2)],
                     q=list(range(PASSES)))

        def step(token):
            kind, arg = token[0], [int(x) for x in token[1:]]
            nxt = order[kind].pop(0) if kind in order else None
            if kind == "w":
                widen(nxt)
            elif kind == "t":
                turn(nxt)
                gather(nxt)
            elif kind == "d":
                d_quantize(nxt)
            elif kind == "s":
                score(nxt)
                sigmoid(nxt)
            elif kind == "e":
                encode(*nxt)
                weigh(*nxt)
            elif kind == "v":
                v_interleave(*nxt, 2, nc.scalar.copy)
            elif kind == "q":
                v_quantize(nxt)
            elif kind == "c":
                widen_only(arg[0], nc.vector.tensor_copy)
            elif kind == "C":
                widen_only(arg[0], nc.scalar.copy)
            elif kind == "T":
                turn(arg[0])
            elif kind == "p":
                scale_turned(arg[0])
            elif kind == "l":
                lam_mult(arg[0], arg[1], 4 if arg[0] == last else 2)
            elif kind == "L":
                lam_quantize(arg[0], arg[1] if arg[0] == last else 0, 4 if arg[0] == last else 1)
            elif kind == "i":
                h_interleave(*arg)
            elif kind == "I":
                h_interleave(*arg, nc.scalar.copy)
            elif kind == "h":
                h_quantize(*arg)
            elif kind == "u":
                update(*arg)
            elif kind == "x":
                nc.vector.tensor_copy(out=ipw_f[:], in_=ipw_bf[:])
            elif kind == "o":
                store(arg[0], arg[1], "scalar")
            elif kind == "O":
                store(arg[0], arg[1], "vector")

        for token in PROGRAM.split():
            step(token)
